import numpy as np
import ml_dtypes


def mxq(x, axis, fmt="e4m3"):
    dtype, down = {"e4m3": (ml_dtypes.float8_e4m3fn, 7), "e5m2": (ml_dtypes.float8_e5m2, 14)}[fmt]
    v = np.moveaxis(np.asarray(x, np.float32).astype(ml_dtypes.bfloat16).astype(np.float64), axis, -1)
    blocks = v.reshape(v.shape[:-1] + (-1, 32))
    amax = np.abs(blocks).max(-1, keepdims=True)
    byte = np.maximum(np.where(amax > 0, np.frexp(amax)[1] - 1 + 127, 0) - down, 1)
    scale = np.exp2(byte - 127.0)
    codes = (blocks / scale).astype(np.float32).astype(dtype).astype(np.float64)
    return np.moveaxis((codes * scale).reshape(v.shape), -1, axis)


WIDE = False


def mx_kscale(k):
    if not WIDE:
        return np.ones(k)
    levels = np.array([10, -10, 5, -5, 0])
    if k % 512:
        return np.exp2(np.random.permutation(np.resize(levels, k // 32))).repeat(32)
    a = np.empty((k // 512, 16))
    for p in range(k // 512):
        a[p, :8] = np.random.permutation(np.resize(levels, 8))
        for g in range(8):
            far = levels[np.abs(levels - a[p, g]) >= 10]
            a[p, g + 8] = far[np.random.randint(len(far))]
    return np.exp2(a.ravel()).repeat(32)


BF16 = ml_dtypes.bfloat16


def bf(x):
    return np.asarray(x, np.float32).astype(BF16)


def f64(x):
    return np.asarray(x).astype(np.float64)

def planes(Y):
    n, m = Y.shape
    b = f64(bf(Y)).reshape(n // 32, 32, m)
    amax = np.abs(b).max(1)
    byte = np.clip(np.where(amax > 0, np.frexp(amax)[1] - 1 + 127 - 7, 1), 1, 254)
    codes = (b * np.exp2(127.0 - byte)[:, None, :]).reshape(n, m).astype(np.float32).astype(ml_dtypes.float8_e4m3fn).view(np.uint8)
    words = codes.reshape(n // 512, 128, 4, m).transpose(0, 1, 3, 2)
    return np.ascontiguousarray(words), np.ascontiguousarray(byte.astype(np.uint8).reshape(n // 512, 16, m))


T, D, E, R = 1024, 1024, 4, 256
ER = E * R


def setup_inputs():
    s, t = mx_kscale(D), mx_kscale(ER).reshape(E, R)
    x0 = bf(np.random.standard_normal((T, D)) * s)
    x = bf(np.random.standard_normal((T, D)) * s)
    v = bf(np.random.standard_normal((D, E, R)) / np.sqrt(D) / s[:, None, None])
    wg = bf(np.random.standard_normal((D, E)) / np.sqrt(D) / s[:, None])
    c = bf((1.0 + 0.1 * np.random.standard_normal((E, R))) * t)
    u = bf(np.random.standard_normal((E, R, D)) * 2.0 / np.sqrt(R) / t[:, :, None])
    b = bf(0.3 * np.random.standard_normal(D) * np.ones(D))
    return {"x0": x0, "x": x, "v": v, "wg": wg, "c": c, "u": u, "b": b}


def core(x0, x, v, wg, c, u, b):
    x0, x, v, wg, c, u, b = f64(x0), f64(x), f64(v), f64(wg), f64(c), f64(u), f64(b)
    t, d = x.shape
    e, r = c.shape
    p = (mxq(x, 1, "e4m3") @ mxq(v.reshape(d, e * r), 0, "e4m3")).reshape(t, e, r)
    a = np.stack([np.sum(x * wg[:, i], axis=1) for i in range(e)], axis=1)
    g = np.exp(a - a.max(axis=-1, keepdims=True))
    g = g / g.sum(axis=-1, keepdims=True)
    h = g[:, :, None] * np.tanh(p) * c[None, :, :]
    z = mxq(h.reshape(t, e * r), 1, "e4m3") @ mxq(u.reshape(e * r, d), 0, "e4m3")
    return x0 * (z + b[None, :]) + x


def reference(x0, x, v, wg, c, u, b):
    R_out = core(x0, x, v, wg, c, u, b)
    words, scales = planes(R_out)
    return R_out, words, scales

from contextlib import ExitStack

import concourse.mybir as mybir
from concourse.masks import make_identity

T, D, E, R = 1024, 1024, 4, 256
FLOPS = 2 * T * D * E * R * 2 + 2 * T * D * E

F32 = mybir.dt.float32
BF16 = mybir.dt.bfloat16
I32 = mybir.dt.int32
U32 = mybir.dt.uint32
U8 = mybir.dt.uint8
FP8X4 = mybir.dt.float8_e4m3fn_x4
ALU = mybir.AluOpType
ACT = mybir.ActivationFunctionType
AXIS = mybir.AxisListType

P = 128
PACK = 4
KP = P * PACK
CHUNKS = T // P
PARTS = 3
SLAB = 256


def tile_dcnmixlowrankcrossexperts_x1_kernel(tc, x0, x, v, wg, c, u, b, out_0, out_1, out_2):
    nc = tc.nc
    v2 = v.rearrange("d e r -> d (e r)")
    u2 = u.rearrange("e r d -> (e r) d")

    with ExitStack() as ctx:
        sb = ctx.enter_context(tc.tile_pool(name="sb", bufs=1))
        ps = ctx.enter_context(tc.psum_pool(name="ps", bufs=1))
        ctx.enter_context(tc.manual_schedule())

        def tile(name, shape, dtype):
            return sb.tile(shape, dtype, name=name, align_bytes=64)

        def ring(name, count, shape, dtype):
            return [tile(name + str(n), shape, dtype) for n in range(count)]

        gate_bank = ps.tile([P, KP], F32, name="gate_bank")
        banks = [ps.tile([P, KP], F32, name="bank" + str(n)) for n in range(7)]
        held = {}
        late_x0 = [(0, 0), (0, 1), (0, 2), (0, 3), (1, 1), (1, 3)]

        def take_bank(key):
            held[key] = banks[len(held)]
            return held[key]

        def empty_bank(key):
            banks.append(held[key])
            return held[key][:]

        ident_f = tile("ident_f", [P, P], F32)
        ident_h = tile("ident_h", [P, P], BF16)
        warm = tile("warm", [P, 1], F32)
        x_sb = tile("x_sb", [P, CHUNKS, D], BF16)
        x0_sb = tile("x0_sb", [P, CHUNKS, D], BF16)
        x0_t = tile("x0_t", [P, 2, 4, KP], F32)
        v_raw = tile("v_raw", [P, 2, 2, PACK, KP], BF16)
        u_raw = tile("u_raw", [P, 2, 2, PACK, KP], BF16)
        wg_raw = tile("wg_raw", [P, 2, PACK * E], BF16)
        wg_neg = tile("wg_neg", [P, 2, PACK, E], BF16)
        c_raw = tile("c_raw", [32, E * R], BF16)
        c_mat = tile("c_mat", [P, 2, PACK, P], BF16)
        expert_mask = tile("expert_mask", [P, E], F32)
        b_col = tile("b_col", [P, 4, 2], BF16)
        x_codes = tile("x_codes", [P, 4, KP], U32)
        x_scales = tile("x_scales", [P, 4, KP], U8)
        v_codes = tile("v_codes", [P, 2, 2, KP], U32)
        v_scales = tile("v_scales", [P, 2, 2, KP], U8)
        u_codes = tile("u_codes", [P, 4, KP], U32)
        u_scales = tile("u_scales", [P, 4, KP], U8)
        h_codes = tile("h_codes", [P, 4, KP], U32)
        h_scales = tile("h_scales", [P, 4, KP], U8)
        o_codes = tile("o_codes", [P, 2, D], U32)
        o_scales = tile("o_scales", [P, 2, D], U8)
        neg_max = tile("neg_max", [P, CHUNKS], F32)
        expo = tile("expo", [P, CHUNKS, E], F32)
        total = tile("total", [P, CHUNKS], F32)
        inverse = tile("inverse", [P, CHUNKS], F32)
        gate = tile("gate", [P, CHUNKS, E], F32)
        rest = tile("rest", [P, CHUNKS, E], F32)
        gate_parts = tile("gate_parts", [P, CHUNKS, P], BF16)
        gate_t = tile("gate_t", [P, CHUNKS, P], BF16)
        x_group = ring("x_group", 2, [P, 2, 2, P, PACK], BF16)
        v_group = ring("v_group", 4, [P, PACK, P, PACK], BF16)
        u_group = ring("u_group", 2, [P, 2, 2, P, PACK], BF16)
        tanh_p = ring("tanh_p", 2, [P, 2, 2 * P, 2], F32)
        h_group = ring("h_group", 2, [P, 2, 2, P, PACK], BF16)
        cross_t = ring("cross_t", 4, [P, KP], F32)
        o_f32 = ring("o_f32", 4, [P, PACK, SLAB], F32)
        o_group = tile("o_group", [P, D, PACK], BF16)

        def copy_on(engine, out, in_):
            if engine == "act":
                nc.scalar.copy(out=out, in_=in_)
            elif engine == "pool":
                nc.gpsimd.tensor_scalar(out=out, in0=in_, scalar1=1.0, scalar2=0.0, op0=ALU.mult, op1=ALU.add)
            else:
                nc.vector.tensor_copy(out=out, in_=in_)

        def quantize(codes, scales, grouped):
            nc.vector.quantize_mx(out=codes.bitcast(FP8X4), scales=scales, in_=grouped)

        def load_small():
            nc.scalar.dma_start(out=c_raw[:], in_=c.rearrange("e r -> (e r)").partition_broadcast(32))
            nc.scalar.dma_start(out=wg_raw[:], in_=wg.rearrange("(g p j) e -> p g (j e)", g=2, j=PACK))

        def load_b():
            nc.sync.dma_start(out=b_col[:], in_=b.rearrange("(i p e) -> p i e", i=4, e=2))

        def token_rows(ap, group):
            return ap[KP * group : KP * (group + 1), :].rearrange("(p t) d -> p t d", t=PACK)

        def load_x(first, count):
            group, t = divmod(first, PACK)
            nc.sync.dma_start(out=x_sb[:, first : first + count, :], in_=token_rows(x, group)[:, t : t + count, :])

        def load_x0(group):
            nc.sync.dma_start(out=x0_sb[:, PACK * group : PACK * (group + 1), :], in_=token_rows(x0, group))

        def load_v(g, ge):
            rows = v2[KP * g : KP * (g + 1), KP * ge : KP * (ge + 1)]
            nc.sync.dma_start(out=v_raw[:, g, ge, :, :], in_=rows.rearrange("(p j) n -> p j n", j=PACK))

        def load_u(ge, half):
            rows = u2[KP * ge : KP * (ge + 1), KP * half : KP * (half + 1)]
            nc.sync.dma_start(out=u_raw[:, ge, half, :, :], in_=rows.rearrange("(p j) n -> p j n", j=PACK))

        def setup():
            nc.vector.memset(warm[:], 0.0)
            nc.scalar.activation(out=warm[:], in_=warm[:], func=ACT.Exp)
            make_identity(nc, ident_f[:])
            make_identity(nc, ident_h[:])
            nc.vector.memset(c_mat[:].rearrange("p g j m -> p (g j m)").bitcast(I32), 0)
            nc.vector.memset(gate_parts[:].rearrange("p n k -> p (n k)").bitcast(I32), 0)
            nc.vector.tensor_reduce(
                out=expert_mask[:],
                in_=ident_h[:, 0 : PARTS * E].rearrange("p (a e) -> p e a", e=E),
                axis=AXIS.X,
                op=ALU.add,
            )

        def constants():
            nc.vector.tensor_scalar(
                out=wg_neg[:].rearrange("p g j e -> p g (j e)"),
                in0=wg_raw[:],
                scalar1=-1.0,
                scalar2=None,
                op0=ALU.mult,
            )
            for ge in range(2):
                nc.vector.tensor_tensor(
                    out=c_mat[0:32, ge, :, :].rearrange("k j (h q) -> k h j q", h=2),
                    in0=c_raw[:, KP * ge : KP * (ge + 1)].rearrange("k (h q j) -> k h j q", h=2, j=PACK),
                    in1=expert_mask[0:32, 2 * ge : 2 * ge + 2].unsqueeze(2).unsqueeze(3).to_broadcast([32, 2, PACK, 64]),
                    op=ALU.mult,
                )

        def x_turn(n):
            bank = take_bank(("x", n))
            words = x_sb[:, n, :].bitcast(F32)
            for g in range(2):
                for w in range(2):
                    col = P * (2 * g + w)
                    nc.tensor.transpose(bank[:, col : col + P], words[:, 256 * g + w : 256 * (g + 1) : 2], ident_f[:])

        def x_copy(n, engine="act"):
            dst = x_group[n // 2 % 2][:].rearrange("p g n r j -> p (g n r j)").bitcast(F32)
            copy_on(
                engine,
                dst.rearrange("p (g n r w) -> p g n r w", g=2, n=2, w=2)[:, :, n % 2, :, :],
                empty_bank(("x", n)).rearrange("p (g w r) -> p g r w", g=2, w=2),
            )

        def x_quant(pair):
            grouped = x_group[pair % 2][:].rearrange("p g n r j -> p (g n r j)")
            quantize(x_codes[:, pair, :], x_scales[:, pair, :], grouped)

        def logits(n):
            for g in range(2):
                for j in range(PACK):
                    nc.tensor.matmul(
                        out=gate_bank[:, E * n : E * (n + 1)],
                        lhsT=x_group[n // 2 % 2][:, g, n % 2, :, j],
                        rhs=wg_neg[:, g, j, :],
                        start=(g == 0 and j == 0),
                        stop=(g == 1 and j == PACK - 1),
                    )

        def gate_max(lo, hi):
            nc.vector.tensor_reduce(
                out=neg_max[:, lo:hi],
                in_=gate_bank[:, E * lo : E * hi].rearrange("p (n e) -> p n e", e=E),
                axis=AXIS.X,
                op=ALU.min,
            )

        def gate_exp(lo, hi):
            for n in range(lo, hi):
                nc.scalar.activation(
                    out=expo[:, n, :],
                    in_=gate_bank[:, E * n : E * (n + 1)],
                    func=ACT.Exp,
                    scale=-1.0,
                    bias=neg_max[:, n : n + 1],
                    accum_out=total[:, n : n + 1],
                )

        def gate_inverse(lo, hi):
            nc.vector.reciprocal(out=inverse[:, lo:hi], in_=total[:, lo:hi])

        def gate_high(lo, hi):
            spread = inverse[:, lo:hi].unsqueeze(2).to_broadcast([P, hi - lo, E])
            nc.vector.tensor_tensor(out=gate[:, lo:hi, :], in0=expo[:, lo:hi, :], in1=spread, op=ALU.mult)
            nc.vector.tensor_tensor(out=gate_parts[:, lo:hi, 0:E], in0=expo[:, lo:hi, :], in1=spread, op=ALU.mult)

        def gate_mid(lo, hi):
            high = gate_parts[:, lo:hi, 0:E]
            nc.vector.tensor_tensor(out=rest[:, lo:hi, :], in0=gate[:, lo:hi, :], in1=high, op=ALU.subtract)
            nc.vector.tensor_tensor(
                out=gate_parts[:, lo:hi, E : 2 * E], in0=gate[:, lo:hi, :], in1=high, op=ALU.subtract
            )

        def gate_low(lo, hi):
            nc.vector.tensor_tensor(
                out=gate_parts[:, lo:hi, 2 * E : 3 * E],
                in0=rest[:, lo:hi, :],
                in1=gate_parts[:, lo:hi, E : 2 * E],
                op=ALU.subtract,
            )

        def gate_turn(lo, hi):
            bank = take_bank(("g", lo))[:].bitcast(BF16)
            for n in range(lo, hi):
                nc.tensor.transpose(bank[:, P * (n - lo) : P * (n - lo + 1)], gate_parts[:, n, :], ident_h[:])

        def gate_copy(lo, hi):
            nc.scalar.copy(
                out=gate_t[:, lo:hi, :].rearrange("p n r -> p (n r)"),
                in_=empty_bank(("g", lo)).bitcast(BF16)[:, 0 : P * (hi - lo)],
            )

        def v_weave(g, ge, lo, hi, engine):
            copy_on(
                engine,
                v_group[2 * ge + g][:, lo:hi, :, :],
                v_raw[:, g, ge, :, :].rearrange("p k (m j) -> p j m k", j=PACK)[:, lo:hi, :, :],
            )

        def v_quant(g, ge):
            quantize(v_codes[:, g, ge, :], v_scales[:, g, ge, :], v_group[2 * ge + g][:].rearrange("p j m k -> p (j m k)"))

        def u_weave(ge, i, engine):
            copy_on(
                engine,
                u_group[i % 2][:, ge, :, :, :].rearrange("p e (a q) k -> p a k q e", q=2),
                u_raw[:, ge, i // 2, :, SLAB * (i % 2) : SLAB * (i % 2 + 1)].rearrange("p k (a q e) -> p a k q e", q=2, e=2),
            )

        def u_quant(i):
            quantize(u_codes[:, i, :], u_scales[:, i, :], u_group[i % 2][:].rearrange("p g e q k -> p (g e q k)"))

        def down(pair, ge, jh):
            bank = take_bank(("p", pair, ge, jh))
            for jj in range(2):
                cols = slice(P * (2 * jh + jj), P * (2 * jh + jj + 1))
                for g in range(2):
                    nc.tensor.matmul_mx(
                        out=bank[:, 2 * P * jj : 2 * P * (jj + 1)],
                        lhsT=v_codes[:, g, ge, cols].bitcast(FP8X4),
                        lhsT_scale=v_scales[:, g, ge, cols],
                        rhs=x_codes[:, pair, 2 * P * g : 2 * P * (g + 1)].bitcast(FP8X4),
                        rhs_scale=x_scales[:, pair, 2 * P * g : 2 * P * (g + 1)],
                        start=(g == 0),
                        stop=(g == 1),
                    )

        def factor(n, ge):
            bank = take_bank(("f", n, ge))
            for j in range(PACK):
                nc.tensor.matmul(
                    out=bank[:, P * j : P * (j + 1)],
                    lhsT=c_mat[:, ge, j, :],
                    rhs=gate_t[:, n, :],
                    start=True,
                    stop=True,
                )

        def squash(pair, ge, jh):
            nc.scalar.activation(
                out=tanh_p[ge][:, jh, :, :],
                in_=empty_bank(("p", pair, ge, jh)).rearrange("p (j r) -> p r j", j=2),
                func=ACT.Tanh,
            )

        def h_mul(n, ge):
            rows = slice(P * (n % 2), P * (n % 2 + 1))
            nc.vector.tensor_tensor(
                out=h_group[n // 2 % 2][:, ge, n % 2, :, :].rearrange("p r (a j) -> p r a j", a=2),
                in0=empty_bank(("f", n, ge)).rearrange("p (a j r) -> p r a j", a=2, j=2),
                in1=tanh_p[ge][:, :, rows, :].rearrange("p a r j -> p r a j"),
                op=ALU.mult,
            )

        def h_quant(pair):
            grouped = h_group[pair % 2][:].rearrange("p g n r j -> p (g n r j)")
            quantize(h_codes[:, pair, :], h_scales[:, pair, :], grouped)

        def x0_turn(group, i):
            bank = take_bank(("x0", group, i))
            for t in range(PACK):
                words = x0_sb[:, PACK * group + t, :].bitcast(F32)
                nc.tensor.transpose(bank[:, P * t : P * (t + 1)], words[:, P * i : P * (i + 1)], ident_f[:])

        def x0_copy(group, i):
            nc.scalar.copy(out=x0_t[:, group, i, :], in_=empty_bank(("x0", group, i)))

        def up(group, i, e):
            bank = take_bank(("z", group, i, e))
            for half in range(2):
                for ge in range(2):
                    cols = slice(SLAB * ge + P * e, SLAB * ge + P * (e + 1))
                    rows = slice(2 * P * ge, 2 * P * (ge + 1))
                    nc.tensor.matmul_mx(
                        out=bank[:, 2 * P * half : 2 * P * (half + 1)],
                        lhsT=u_codes[:, i, cols].bitcast(FP8X4),
                        lhsT_scale=u_scales[:, i, cols],
                        rhs=h_codes[:, 2 * group + half, rows].bitcast(FP8X4),
                        rhs_scale=h_scales[:, 2 * group + half, rows],
                        start=(ge == 0),
                        stop=(ge == 1),
                    )

        def cross(group, i, e):
            if (group, i) in late_x0:
                nc.scalar.activation(
                    out=cross_t[(2 * i + e) % 4][:],
                    in_=empty_bank(("z", group, i, e)),
                    func=ACT.Identity,
                    bias=b_col[:, i, e : e + 1],
                )
                return
            pairs = x0_t[:, group, i, :].bitcast(BF16).rearrange("p (r e) -> p r e", e=2)
            nc.vector.scalar_tensor_tensor(
                out=cross_t[(2 * i + e) % 4][:],
                in0=empty_bank(("z", group, i, e)),
                scalar=b_col[:, i, e : e + 1],
                in1=pairs[:, :, e],
                op0=ALU.add,
                op1=ALU.mult,
            )

        def back(group, i, half):
            bank = take_bank(("o", group, i, half))
            for t in range(2):
                for e in range(2):
                    col = P * (2 * t + e)
                    tok = P * (2 * half + t)
                    nc.tensor.transpose(bank[:, col : col + P], cross_t[(2 * i + e) % 4][:, tok : tok + P], ident_f[:])

        def residual(group, i, half):
            first = PACK * group + 2 * half
            late = (group, i) in late_x0
            other = x0_sb if late else x_sb
            nc.vector.tensor_tensor(
                out=o_f32[i][:, 2 * half : 2 * half + 2, :].rearrange("p t (q e) -> p t q e", e=2),
                in0=empty_bank(("o", group, i, half)).rearrange("p (t e q) -> p t q e", t=2, e=2),
                in1=other[:, first : first + 2, SLAB * i : SLAB * (i + 1)].rearrange("p t (q e) -> p t q e", e=2),
                op=ALU.mult if late else ALU.add,
            )

        def plus(group, i, half, engine):
            first = PACK * group + 2 * half
            rows = o_f32[i][:, 2 * half : 2 * half + 2, :]
            queue = nc.gpsimd if engine == "pool" else nc.vector
            queue.tensor_tensor(out=rows, in0=rows, in1=x_sb[:, first : first + 2, SLAB * i : SLAB * (i + 1)], op=ALU.add)

        def store_out(group, i):
            nc.sync.dma_start(out=token_rows(out_0, group)[:, :, SLAB * i : SLAB * (i + 1)], in_=o_f32[i][:])

        def o_weave(group, i, engine):
            copy_on(
                engine,
                o_group[:, SLAB * i : SLAB * (i + 1), :].rearrange("p (a m) t -> p a t m", m=4),
                o_f32[i][:].rearrange("p t (a m) -> p a t m", m=4),
            )

        def o_quant(group, lo, hi):
            cols = slice(SLAB * lo, SLAB * hi)
            grouped = o_group[:, cols, :].rearrange("p m t -> p (m t)")
            quantize(o_codes[:, group, cols], o_scales[:, group, cols], grouped)

        def store_codes(group, lo, hi):
            cols = slice(SLAB * lo, SLAB * hi)
            nc.sync.dma_start(
                out=out_1[group].rearrange("p m t -> p (m t)").bitcast(I32)[:, cols],
                in_=o_codes[:, group, cols].bitcast(I32),
            )

        def store_scales(group):
            for q in range(4):
                queue = nc.scalar if group == 1 and q % 2 else nc.sync
                queue.dma_start(
                    out=out_2[group, 4 * q : 4 * q + 4, :].bitcast(I32),
                    in_=o_scales[32 * q : 32 * q + 4, group, :].bitcast(I32),
                )

        order = [
            (load_small,), (load_x, 2, 2), (load_x, 1, 1), (load_x, 0, 1), (load_v, 1, 0),
            (setup,), (constants,), (load_v, 0, 0), (x_turn, 2), (v_weave, 1, 0, 0, 2, "dve"),
            (load_x, 4, 4), (x_turn, 3), (v_weave, 1, 0, 2, 4, "dve"), (x_turn, 1), (x_copy, 3),
            (load_v, 0, 1), (v_weave, 0, 0, 2, 4, "dve"), (x_turn, 0), (x_copy, 2), (logits, 3),
            (x_copy, 1), (logits, 1), (load_v, 1, 1), (x_copy, 0), (load_u, 1, 0),
            (logits, 2), (logits, 0), (x_quant, 0), (load_u, 0, 0), (x_turn, 5),
            (v_weave, 0, 0, 0, 2, "act"), (load_x0, 1), (x_turn, 4), (load_x0, 0), (v_quant, 1, 0),
            (gate_max, 0, 4), (x_turn, 7), (gate_exp, 0, 4), (x_copy, 5), (x_quant, 1),
            (x_copy, 4), (gate_inverse, 0, 4), (v_quant, 0, 0), (gate_high, 0, 4), (down, 0, 0, 1),
            (v_weave, 1, 1, 2, 4, "act"), (v_weave, 0, 1, 2, 4, "dve"), (down, 0, 0, 0), (x_copy, 7), (v_weave, 0, 1, 0, 2, "dve"),
            (gate_mid, 0, 4), (v_weave, 1, 1, 0, 2, "dve"), (v_quant, 0, 1), (load_u, 1, 1), (gate_low, 0, 4),
            (logits, 5), (logits, 4), (v_quant, 1, 1), (u_weave, 1, 1, "dve"), (x_turn, 6),
            (gate_turn, 0, 4), (u_weave, 1, 0, "dve"), (squash, 0, 0, 0), (squash, 0, 0, 1), (gate_copy, 0, 4),
            (x_copy, 6), (u_weave, 0, 0, "dve"), (logits, 7), (x_quant, 2), (down, 0, 1, 0),
            (x_quant, 3), (down, 0, 1, 1), (u_weave, 0, 1, "act"), (logits, 6), (load_u, 0, 1),
            (factor, 0, 0), (factor, 1, 0), (squash, 0, 1, 1), (factor, 0, 1), (factor, 3, 0),
            (squash, 0, 1, 0), (gate_max, 4, 8), (h_mul, 1, 0), (factor, 2, 0), (gate_exp, 4, 8),
            (h_mul, 0, 0), (gate_inverse, 4, 8), (h_mul, 0, 1), (factor, 1, 1), (gate_high, 4, 8),
            (down, 1, 0, 0), (h_mul, 1, 1), (down, 1, 0, 1), (down, 1, 1, 0), (gate_mid, 4, 8),
            (squash, 1, 0, 0), (down, 1, 1, 1), (squash, 1, 0, 1), (squash, 1, 1, 0), (u_quant, 0),
            (squash, 1, 1, 1), (down, 2, 0, 1), (gate_low, 4, 8), (h_mul, 2, 0), (factor, 2, 1),
            (gate_turn, 4, 8), (h_mul, 2, 1), (x0_turn, 1, 2), (u_weave, 1, 2, "act"), (h_mul, 3, 0),
            (factor, 3, 1), (h_mul, 3, 1), (h_quant, 0), (x0_copy, 1, 2), (h_quant, 1),
            (down, 2, 0, 0), (gate_copy, 4, 8), (down, 2, 1, 0), (down, 2, 1, 1), (load_b,),
            (factor, 4, 0), (u_quant, 1), (u_weave, 0, 2, "dve"), (factor, 4, 1), (squash, 2, 0, 0),
            (down, 3, 1, 0), (squash, 2, 0, 1), (squash, 2, 1, 0), (up, 0, 0, 1), (squash, 2, 1, 1),
            (cross, 0, 0, 1), (up, 0, 1, 0), (up, 0, 1, 1), (h_mul, 4, 0), (down, 3, 0, 1),
            (cross, 0, 1, 0), (h_mul, 4, 1), (up, 0, 0, 0), (factor, 5, 1), (cross, 0, 1, 1),
            (back, 0, 1, 1), (factor, 5, 0), (u_quant, 2), (u_weave, 1, 3, "dve"), (u_weave, 0, 3, "act"),
            (h_mul, 5, 1), (down, 3, 1, 1), (h_mul, 5, 0), (down, 3, 0, 0), (cross, 0, 0, 0),
            (factor, 7, 0), (residual, 0, 1, 1), (back, 0, 1, 0), (squash, 3, 1, 1), (u_quant, 3),
            (squash, 3, 1, 0), (residual, 0, 1, 0), (squash, 3, 0, 1), (back, 0, 0, 0), (back, 0, 0, 1),
            (plus, 0, 1, 1, "pool"), (residual, 0, 0, 1), (plus, 0, 1, 0, "pool"), (squash, 3, 0, 0), (x0_turn, 1, 0),
            (residual, 0, 0, 0), (factor, 7, 1), (up, 0, 3, 0), (x0_copy, 1, 0), (up, 0, 3, 1),
            (h_mul, 7, 1), (cross, 0, 3, 0), (cross, 0, 3, 1), (factor, 6, 1), (factor, 6, 0),
            (h_mul, 7, 0), (up, 0, 2, 0), (store_out, 0, 1), (up, 0, 2, 1), (back, 0, 3, 0),
            (cross, 0, 2, 0), (cross, 0, 2, 1), (back, 0, 3, 1), (o_weave, 0, 1, "act"), (h_mul, 6, 1),
            (back, 0, 2, 1), (h_mul, 6, 0), (back, 0, 2, 0), (h_quant, 2), (h_quant, 3),
            (up, 1, 0, 0), (residual, 0, 3, 0), (up, 1, 0, 1), (residual, 0, 2, 0), (plus, 0, 0, 1, "pool"),
            (plus, 0, 0, 0, "pool"), (plus, 0, 3, 0, "pool"), (up, 1, 1, 1), (o_weave, 0, 0, "act"), (residual, 0, 2, 1),
            (up, 1, 1, 0), (residual, 0, 3, 1), (up, 1, 3, 1), (up, 1, 3, 0), (cross, 1, 0, 1),
            (store_out, 0, 0), (plus, 0, 3, 1, "dve"), (cross, 1, 1, 1), (cross, 1, 1, 0), (back, 1, 1, 1),
            (o_weave, 0, 3, "act"), (back, 1, 1, 0), (cross, 1, 0, 0), (o_quant, 0, 0, 2), (back, 1, 0, 1),
            (back, 1, 0, 0), (plus, 0, 2, 1, "pool"), (cross, 1, 3, 0), (plus, 0, 2, 0, "pool"), (residual, 1, 1, 1),
            (up, 1, 2, 0), (up, 1, 2, 1), (store_out, 0, 3), (plus, 1, 1, 1, "pool"), (store_codes, 0, 0, 2),
            (residual, 1, 1, 0), (residual, 1, 0, 0), (cross, 1, 3, 1), (residual, 1, 0, 1), (cross, 1, 2, 0),
            (back, 1, 3, 1), (o_weave, 0, 2, "act"), (plus, 1, 1, 0, "pool"), (cross, 1, 2, 1), (o_weave, 1, 1, "act"),
            (back, 1, 2, 0), (o_quant, 0, 2, 4), (store_out, 0, 2), (store_out, 1, 0), (back, 1, 2, 1),
            (store_out, 1, 1), (back, 1, 3, 0), (residual, 1, 3, 1), (o_weave, 1, 0, "act"), (residual, 1, 2, 0),
            (store_scales, 0), (residual, 1, 2, 1), (store_codes, 0, 2, 4), (o_weave, 1, 2, "act"), (plus, 1, 3, 1, "pool"),
            (residual, 1, 3, 0), (o_quant, 1, 0, 2), (plus, 1, 3, 0, "dve"), (o_weave, 1, 3, "dve"), (store_out, 1, 2),
            (o_quant, 1, 2, 3), (store_codes, 1, 0, 2), (store_out, 1, 3), (store_codes, 1, 2, 3), (o_quant, 1, 3, 4),
            (store_codes, 1, 3, 4), (store_scales, 1),
        ]

        for step, *args in order:
            step(*args)
